import numpy as np
import ml_dtypes


def mxq(x, axis, fmt="e4m3"):
    dtype, down = {"e4m3": (ml_dtypes.float8_e4m3fn, 7), "e5m2": (ml_dtypes.float8_e5m2, 14)}[fmt]
    v = np.moveaxis(np.asarray(x, np.float32).astype(ml_dtypes.bfloat16).astype(np.float64), axis, -1)
    blocks = v.reshape(v.shape[:-1] + (-1, 32))
    amax = np.abs(blocks).max(-1, keepdims=True)
    byte = np.maximum(np.where(amax > 0, np.frexp(amax)[1] - 1 + 127, 0) - down, 1)
    scale = np.exp2(byte - 127.0)
    codes = (blocks / scale).astype(np.float32).astype(dtype).astype(np.float64)
    return np.moveaxis((codes * scale).reshape(v.shape), -1, axis)


WIDE = False


def mx_kscale(k):
    if not WIDE:
        return np.ones(k)
    levels = np.array([10, -10, 5, -5, 0])
    if k % 512:
        return np.exp2(np.random.permutation(np.resize(levels, k // 32))).repeat(32)
    a = np.empty((k // 512, 16))
    for p in range(k // 512):
        a[p, :8] = np.random.permutation(np.resize(levels, 8))
        for g in range(8):
            far = levels[np.abs(levels - a[p, g]) >= 10]
            a[p, g + 8] = far[np.random.randint(len(far))]
    return np.exp2(a.ravel()).repeat(32)


def f64(x):
    return np.asarray(x).astype(np.float64)


def striped(idx):
    return np.tile(idx.reshape(-1, 16).T, (8, 1)).astype(np.uint16)


def unstriped(offs):
    return offs[:16].T.reshape(-1).astype(np.int64)


def striped8(idx):
    return np.concatenate([x.reshape(-1, 16).T for x in idx]).astype(np.uint16)


def runs(offs, k):
    lists = np.stack([offs[16 * r : 16 * r + 16].T.reshape(-1) for r in range(8)]).astype(np.int64)
    return lists[np.arange(k) % 512 // 64]


def pack_weight(w):
    k, n = w.shape
    w = f64(np.asarray(w, np.float32).astype(ml_dtypes.bfloat16)).reshape(k // 32, 32, n)
    amax = np.abs(w).max(1)
    byte = np.clip(np.where(amax > 0, np.frexp(amax)[1] - 1 + 127 - 7, 1), 1, 254)
    scaled = (w * np.exp2(127.0 - byte)[:, None, :]).reshape(k, n).astype(np.float32)
    words = np.ascontiguousarray(scaled.reshape(k // 512, 128, 4, n).transpose(0, 1, 3, 2)).astype(ml_dtypes.float8_e4m3fn).view(np.uint8)
    return words, np.ascontiguousarray(byte.astype(np.uint8).reshape(k // 512, 16, n))


def unpack_weight(words, scales):
    g, p, n, _ = words.shape
    vals = np.ascontiguousarray(words).view(ml_dtypes.float8_e4m3fn).astype(np.float64) * np.repeat(np.exp2(scales.astype(np.float64) - 127.0), 8, axis=1)[..., None]
    return vals.transpose(0, 1, 3, 2).reshape(g * 512, n)


def sigmoid(v):
    return 1.0 / (1.0 + np.exp(-np.maximum(v, -700.0)))

def planes(y):
    n, m = y.shape
    v = y.astype(np.float32).astype(ml_dtypes.bfloat16).astype(np.float64).reshape(n // 32, 32, m)
    top = np.abs(v).max(1)
    byte = np.clip(np.where(top > 0, np.frexp(top)[1] - 1 + 127 - 7, 1), 1, 254)
    codes = (v * np.exp2(127.0 - byte)[:, None, :]).reshape(n, m).astype(np.float32).astype(ml_dtypes.float8_e4m3fn).view(np.uint8)
    words = codes.reshape(n // 512, 128, 4, m).transpose(0, 1, 3, 2)
    return np.ascontiguousarray(words), np.ascontiguousarray(byte.astype(np.uint8).reshape(n // 512, 16, m))


K, T, S, H, C = 512, 2048, 512, 512, 512


def setup_inputs():
    n = np.random.standard_normal
    s = mx_kscale(K)[:, None]
    packed_xT = pack_weight(n((K, T)) * s)
    packed_w1 = pack_weight(n((K, H)) / np.sqrt(K) / s)
    packed_w2 = pack_weight(n((K, H)) / np.sqrt(K) / s)
    return {
        "x_words": packed_xT[0],
        "x_scales": packed_xT[1],
        "w1_words": packed_w1[0],
        "w1_scales": packed_w1[1],
        "w2_words": packed_w2[0],
        "w2_scales": packed_w2[1],
        "gs": (np.random.uniform(0.5, 1.5, (K, 1)) / s).astype(np.float32),
        "offs": striped(np.random.permutation(T)[:S]),
        "two": striped(np.random.permutation(T)[:S]),
        "n1": striped8(np.stack([np.random.permutation(S) for _ in range(8)])),
        "n2": striped8(np.stack([np.random.permutation(S) for _ in range(8)])),
        "cand": striped(np.random.permutation(T)[:C]),
        "n3": striped8(np.stack([np.random.permutation(S) for _ in range(8)])),
        "n4": striped8(np.stack([np.random.permutation(S) for _ in range(8)])),
    }


def reference(x_words, x_scales, w1_words, w1_scales, w2_words, w2_scales, gs, offs, two, n1, n2, cand, n3, n4):
    x_cand = unpack_weight(x_words, x_scales)[:, unstriped(cand)]
    xq = unpack_weight(x_words, x_scales)[:, unstriped(offs)]
    y = unpack_weight(w1_words, w1_scales).T @ xq
    x_two = unpack_weight(x_words, x_scales)[:, unstriped(two)]
    d = unpack_weight(w2_words, w2_scales).T @ x_two
    z = f64(gs) * (y * (np.tanh(d[np.arange(H)[:, None], runs(n1, H)] - (d[np.arange(H)[:, None], runs(n2, H)]))))
    s = 0.0625 * ((x_cand.T @ mxq(z, 0, "e4m3")))
    out_0 = s + (sigmoid(s[np.arange(C)[:, None], runs(n3, C)])) * (s[np.arange(C)[:, None], runs(n4, C)] - s)
    return (out_0,) + planes(out_0)

@@ -1,0 +1,240 @@
+from contextlib import ExitStack
+
+import concourse.mybir as mybir
+
+K, T, S, H, C = 512, 2048, 512, 512, 512
+FLOPS = 3 * 2 * 512 * 512 * 512
+
+F32 = mybir.dt.float32
+BF16 = mybir.dt.bfloat16
+I32 = mybir.dt.int32
+U32 = mybir.dt.uint32
+U16 = mybir.dt.uint16
+U8 = mybir.dt.uint8
+FP8X4 = mybir.dt.float8_e4m3fn_x4
+ALU = mybir.AluOpType
+ACT = mybir.ActivationFunctionType
+
+P = 128
+PACK = 4
+
+
+def tile_picked_twcjointbtrack_none_po_kernel(tc, x_words, x_scales, w1_words, w1_scales, w2_words, w2_scales, gs, offs, two, n1, n2, cand, n3, n4, out_0, out_1, out_2):
+    nc = tc.nc
+    with ExitStack() as ctx:
+        lists = ctx.enter_context(tc.tile_pool(name="lists", bufs=1))
+        sb = ctx.enter_context(tc.tile_pool(name="sb", bufs=1))
+        psum = ctx.enter_context(tc.psum_pool(name="psum", bufs=1))
+
+        def tile(name, shape, dtype, tag=None):
+            return sb.tile(shape, dtype, name=name, tag=tag or name, align_bytes=64)
+
+        def load_list(name, src):
+            t = lists.tile([P, S // 16], U16, name=name)
+            nc.sync.dma_start(t[:], src)
+            return t
+
+        def words_of(src):
+            return src[0].rearrange("p n t -> p (n t)").bitcast(I32)
+
+        def load_scales(dst, src, eng):
+            for q in range(4):
+                eng.dma_start(dst[32 * q : 32 * q + 4, :].bitcast(I32), src[0][4 * q : 4 * q + 4, :].bitcast(I32))
+
+        def cols(lst, c0, n):
+            return lst[:, c0 // 16 : (c0 + n) // 16]
+
+        xs = tile("xs", [P, T], U8)
+        w2s = tile("w2s", [P, H], U8)
+        w1s = tile("w1s", [P, H], U8)
+        nc.vector.memset(w2s[:].bitcast(I32), 0)
+        nc.vector.memset(w1s[:].bitcast(I32), 0)
+        warm_in = tile("warm_in", [P, 1], F32)
+        warm_out = tile("warm_out", [P, 1], F32)
+        nc.vector.memset(warm_in[:], 0.0)
+
+        def load_x_scales(q, eng):
+            rows = x_scales[0][4 * q : 4 * q + 4, :].bitcast(I32)
+            eng.dma_start(xs[32 * q : 32 * q + 32, :].bitcast(I32), rows.partition_broadcast(8))
+
+        two_t = load_list("two_t", two)
+        for q in range(4):
+            load_x_scales(q, nc.scalar if q < 2 else nc.sync)
+        nc.scalar.activation(warm_out[:], warm_in[:], ACT.Sigmoid)
+        xw = tile("xw", [P, T], U32)
+        nc.sync.dma_start(xw[:].bitcast(I32), words_of(x_words))
+        offs_t = load_list("offs_t", offs)
+        cand_t = load_list("cand_t", cand)
+        load_scales(w2s, w2_scales, nc.sync)
+        w2w = tile("w2w", [P, H], U32)
+        nc.sync.dma_start(w2w[:].bitcast(I32), words_of(w2_words))
+        w1w = tile("w1w", [P, H], U32)
+        nc.sync.dma_start(w1w[:].bitcast(I32), words_of(w1_words))
+        n1_t = load_list("n1_t", n1)
+        n2_t = load_list("n2_t", n2)
+        load_scales(w1s, w1_scales, nc.sync)
+        gs_t = tile("gs_t", [P, PACK], F32)
+        nc.sync.dma_start(gs_t[:], gs.rearrange("(p t) o -> p (t o)", t=PACK))
+        n3_t = load_list("n3_t", n3)
+        n4_t = load_list("n4_t", n4)
+
+        def deal(eng, dst, src):
+            eng.tensor_copy(dst.rearrange("p (t m) -> p t m", t=PACK), src.rearrange("p (m t) -> p t m", t=PACK))
+
+        two_s = tile("two_s", [P, S], U8)
+        two_w = tile("two_w", [P, S], U32)
+        offs_s = tile("offs_s", [P, S], U8)
+        cand_s0 = tile("cand_s0", [P, C], U8)
+        cand_s = tile("cand_s", [P, C], U8)
+        w2ds = tile("w2ds", [P, H], U8)
+        w1ds = tile("w1ds", [P, H], U8)
+        w1dw = tile("w1dw", [P, H], U32)
+
+        nc.vector.tensor_copy(two_s[:], xs[:].indirect(two_t[:]))
+        nc.vector.tensor_copy(offs_s[:], xs[:].indirect(offs_t[:]))
+        nc.vector.tensor_copy(two_w[:], xw[:].indirect(two_t[:]))
+        deal(nc.vector, w2ds[:], w2s[:])
+        w2dw = tile("w2dw", [P, H], U32, tag="w2s")
+        deal(nc.vector, w2dw[:].bitcast(I32), w2w[:].bitcast(I32))
+        offs_w = tile("offs_w", [P, S], U32, tag="w2w")
+        nc.vector.tensor_copy(offs_w[:], xw[:].indirect(offs_t[:]))
+        nc.vector.tensor_copy(cand_s0[:], xs[:].indirect(cand_t[:]))
+        deal(nc.vector, w1dw[:].bitcast(I32), w1w[:].bitcast(I32))
+        deal(nc.vector, cand_s[:], cand_s0[:])
+        deal(nc.vector, w1ds[:], w1s[:])
+        cand_w = tile("cand_w", [P, C], U32, tag="w1s")
+        nc.vector.tensor_copy(cand_w[:].rearrange("p (t m) -> p m t", t=PACK), xw[:].indirect(cand_t[:]))
+
+        def mm(out, lw, ls, t, rw, rs):
+            m = slice(t * P, (t + 1) * P)
+            nc.tensor.matmul_mx(out=out, lhsT=lw[:, m].bitcast(FP8X4), lhsT_scale=ls[:, m], rhs=rw.bitcast(FP8X4), rhs_scale=rs, start=True, stop=True)
+
+        lo = [psum.tile([P, 512], F32, name=f"lo{t}") for t in range(PACK)]
+        hi = [psum.tile([P, 512], F32, name=f"hi{t}") for t in range(PACK)]
+        dwin = [tile(f"dwin{t}", [P, S], F32) for t in range(PACK)]
+        swin = [tile(f"swin{t}", [P, S], F32) for t in range(PACK)]
+        yg = tile("yg", [P, PACK, S], F32)
+        for t in range(PACK):
+            mm(lo[t][:], w2dw, w2ds, t, two_w[:], two_s[:])
+            nc.scalar.copy(dwin[t][:], lo[t][:])
+        for t in range(PACK):
+            mm(hi[t][:], w1dw, w1ds, t, offs_w[:], offs_s[:])
+
+        ga = tile("ga", [P, PACK, S], F32)
+        diff = tile("diff", [P, PACK, S], F32)
+        th = tile("th", [P, PACK, S], F32)
+        zb = tile("zb", [P, S * PACK], BF16)
+        zw = tile("zw", [P, S], U32)
+        zs = tile("zs", [P, S], U8)
+
+        def first(t, c0, n):
+            nc.vector.tensor_copy(ga[:, t, c0 : c0 + n], dwin[t][:].indirect(cols(n1_t, c0, n)))
+
+        def second(t, c0, n):
+            nc.vector.tensor_tensor(diff[:, t, c0 : c0 + n], dwin[t][:].indirect(cols(n2_t, c0, n)), ga[:, t, c0 : c0 + n], ALU.subtract)
+            nc.scalar.activation(th[:, t, c0 : c0 + n], diff[:, t, c0 : c0 + n], ACT.Tanh, scale=-1.0)
+
+        def planes(src, c0, n):
+            return src[:, :, c0 : c0 + n].rearrange("p t (c i) -> p c t i", i=4)
+
+        def woven(dst, c0, n):
+            return dst[:, c0 * PACK : (c0 + n) * PACK].rearrange("p (c i t) -> p c t i", i=4, t=PACK)
+
+        def zmul(c0, n):
+            nc.vector.tensor_tensor(woven(zb, c0, n), planes(yg, c0, n), planes(th, c0, n), ALU.mult)
+
+        def quant(w, s, b, c0, n):
+            nc.vector.quantize_mx(out=w[:, c0 : c0 + n].bitcast(FP8X4), scales=s[:, c0 : c0 + n], in_=b[:, c0 * PACK : (c0 + n) * PACK])
+
+        def score(bank, c0, n):
+            for t in range(PACK):
+                mm(bank[t][:, c0 : c0 + n], cand_w, cand_s, t, zw[:, c0 : c0 + n], zs[:, c0 : c0 + n])
+
+        def leave(bank, t, c0, n):
+            nc.scalar.activation(swin[t][:, c0 : c0 + n], bank[t][:, c0 : c0 + n], ACT.Copy, scale=0.0625)
+
+        steps = [(t, c0, 256) for c0 in (0, 256) for t in range(PACK)]
+        first(*steps[0])
+        for i in range(len(steps)):
+            if i + 1 < len(steps):
+                first(*steps[i + 1])
+            if i == len(steps) - 1:
+                zmul(0, 256)
+            second(*steps[i])
+            if i < PACK:
+                nc.scalar.activation(yg[:, i, :], hi[i][:], ACT.Copy, scale=gs_t[:, i : i + 1])
+        quant(zw, zs, zb, 0, 256)
+        score(lo, 0, 256)
+        for t in range(PACK):
+            leave(lo, t, 0, 256)
+        zmul(256, 128)
+        zmul(384, 128)
+        quant(zw, zs, zb, 256, 128)
+        score(hi, 256, 128)
+        quant(zw, zs, zb, 384, 128)
+        score(hi, 384, 128)
+
+        sg = tile("sg", [P, PACK, S], F32)
+        pa = tile("pa", [P, PACK, S], F32)
+        pu = tile("pu", [P, PACK, S], F32)
+        res = tile("res", [P, PACK, S], F32)
+        rb = tile("rb", [P, S * PACK], BF16)
+        rw = tile("rw", [P, S], U32)
+        rs = tile("rs", [P, S], U8)
+        out_rows = out_0.rearrange("(p t) c -> p t c", t=PACK)
+        out_words = words_of(out_1)
+
+        def gate(t, c0, n):
+            nc.scalar.activation(sg[:, t, c0 : c0 + n], swin[t][:].indirect(cols(n3_t, c0, n)), ACT.Sigmoid)
+
+        def keep(t, c0, n):
+            nc.vector.scalar_tensor_tensor(pu[:, t, c0 : c0 + n], sg[:, t, c0 : c0 + n], 1.0, swin[t][:, c0 : c0 + n], ALU.subtract, ALU.mult)
+
+        def take(t, c0, n):
+            nc.vector.tensor_tensor(pa[:, t, c0 : c0 + n], swin[t][:].indirect(cols(n4_t, c0, n)), sg[:, t, c0 : c0 + n], ALU.mult)
+
+        def join(t0, t1, c0, n):
+            nc.vector.tensor_tensor(res[:, t0:t1, c0 : c0 + n], pa[:, t0:t1, c0 : c0 + n], pu[:, t0:t1, c0 : c0 + n], ALU.subtract)
+
+        def store(c0, n):
+            nc.sync.dma_start(out_rows[:, :, c0 : c0 + n], res[:, :, c0 : c0 + n])
+
+        def store_words(c0, n):
+            nc.sync.dma_start(out_words[:, c0 : c0 + n], rw[:, c0 : c0 + n].bitcast(I32))
+
+        chunks = [(0, 256), (256, 128), (384, 128)]
+        for t in range(PACK):
+            leave(hi, t, 256, 256)
+            gate(t, *chunks[0])
+            keep(t, *chunks[0])
+            take(t, *chunks[0])
+        for t in range(PACK):
+            gate(t, *chunks[1])
+            keep(t, *chunks[1])
+            take(t, *chunks[1])
+            if t == 0:
+                join(0, PACK, *chunks[0])
+                store(*chunks[0])
+        for t in range(PACK):
+            gate(t, *chunks[2])
+        nc.scalar.copy(woven(rb, *chunks[0]), planes(res, *chunks[0]))
+        for t in range(PACK):
+            keep(t, *chunks[2])
+            take(t, *chunks[2])
+            if t == 0:
+                join(0, PACK, *chunks[1])
+                store(*chunks[1])
+                nc.scalar.copy(woven(rb, *chunks[1]), planes(res, *chunks[1]))
+            if t == 2:
+                quant(rw, rs, rb, *chunks[0])
+                store_words(*chunks[0])
+        join(0, 3, *chunks[2])
+        join(3, 4, *chunks[2])
+        quant(rw, rs, rb, *chunks[1])
+        store(*chunks[2])
+        nc.vector.tensor_copy(woven(rb, *chunks[2]), planes(res, *chunks[2]))
+        quant(rw, rs, rb, *chunks[2])
+        store_words(256, 256)
+        for q in range(4):
+            eng = nc.scalar if q % 2 == 0 else nc.sync
+            eng.dma_start(out_2[0][4 * q : 4 * q + 4, :].bitcast(I32), rs[32 * q : 32 * q + 4, :].bitcast(I32))

@@ -17,6 +17,8 @@ ACT = mybir.ActivationFunctionType
 
 P = 128
 PACK = 4
+HALF = S // 2
+QUARTER = S // 4
 
 
 def tile_picked_twcjointbtrack_none_po_kernel(tc, x_words, x_scales, w1_words, w1_scales, w2_words, w2_scales, gs, offs, two, n1, n2, cand, n3, n4, out_0, out_1, out_2):
@@ -37,9 +39,9 @@ def tile_picked_twcjointbtrack_none_po_kernel(tc, x_words, x_scales, w1_words, w
         def words_of(src):
             return src[0].rearrange("p n t -> p (n t)").bitcast(I32)
 
-        def load_scales(dst, src, eng):
+        def load_scales(dst, src):
             for q in range(4):
-                eng.dma_start(dst[32 * q : 32 * q + 4, :].bitcast(I32), src[0][4 * q : 4 * q + 4, :].bitcast(I32))
+                nc.sync.dma_start(dst[32 * q : 32 * q + 4, :].bitcast(I32), src[0][4 * q : 4 * q + 4, :].bitcast(I32))
 
         def cols(lst, c0, n):
             return lst[:, c0 // 16 : (c0 + n) // 16]
@@ -47,32 +49,30 @@ def tile_picked_twcjointbtrack_none_po_kernel(tc, x_words, x_scales, w1_words, w
         xs = tile("xs", [P, T], U8)
         w2s = tile("w2s", [P, H], U8)
         w1s = tile("w1s", [P, H], U8)
-        nc.vector.memset(w2s[:].bitcast(I32), 0)
-        nc.vector.memset(w1s[:].bitcast(I32), 0)
         warm_in = tile("warm_in", [P, 1], F32)
         warm_out = tile("warm_out", [P, 1], F32)
         nc.vector.memset(warm_in[:], 0.0)
-
-        def load_x_scales(q, eng):
-            rows = x_scales[0][4 * q : 4 * q + 4, :].bitcast(I32)
-            eng.dma_start(xs[32 * q : 32 * q + 32, :].bitcast(I32), rows.partition_broadcast(8))
+        nc.vector.memset(w2s[:].bitcast(I32), 0)
+        nc.vector.memset(w1s[:].bitcast(I32), 0)
 
         two_t = load_list("two_t", two)
         for q in range(4):
-            load_x_scales(q, nc.scalar if q < 2 else nc.sync)
+            rows = x_scales[0][4 * q : 4 * q + 4, :].bitcast(I32)
+            eng = nc.scalar if q < 2 else nc.sync
+            eng.dma_start(xs[32 * q : 32 * q + 32, :].bitcast(I32), rows.partition_broadcast(8))
         nc.scalar.activation(warm_out[:], warm_in[:], ACT.Sigmoid)
         xw = tile("xw", [P, T], U32)
         nc.sync.dma_start(xw[:].bitcast(I32), words_of(x_words))
         offs_t = load_list("offs_t", offs)
         cand_t = load_list("cand_t", cand)
-        load_scales(w2s, w2_scales, nc.sync)
         w2w = tile("w2w", [P, H], U32)
         nc.sync.dma_start(w2w[:].bitcast(I32), words_of(w2_words))
+        load_scales(w2s, w2_scales)
         w1w = tile("w1w", [P, H], U32)
         nc.sync.dma_start(w1w[:].bitcast(I32), words_of(w1_words))
         n1_t = load_list("n1_t", n1)
         n2_t = load_list("n2_t", n2)
-        load_scales(w1s, w1_scales, nc.sync)
+        load_scales(w1s, w1_scales)
         gs_t = tile("gs_t", [P, PACK], F32)
         nc.sync.dma_start(gs_t[:], gs.rearrange("(p t) o -> p (t o)", t=PACK))
         n3_t = load_list("n3_t", n3)
@@ -84,26 +84,24 @@ def tile_picked_twcjointbtrack_none_po_kernel(tc, x_words, x_scales, w1_words, w
         two_s = tile("two_s", [P, S], U8)
         two_w = tile("two_w", [P, S], U32)
         offs_s = tile("offs_s", [P, S], U8)
+        offs_w = tile("offs_w", [P, S], U32)
         cand_s0 = tile("cand_s0", [P, C], U8)
         cand_s = tile("cand_s", [P, C], U8)
         w2ds = tile("w2ds", [P, H], U8)
+        w2dw = tile("w2dw", [P, H], U32)
         w1ds = tile("w1ds", [P, H], U8)
         w1dw = tile("w1dw", [P, H], U32)
 
+        deal(nc.gpsimd, w2dw[:].bitcast(I32), w2w[:].bitcast(I32))
+        deal(nc.gpsimd, w2ds[:], w2s[:])
+        deal(nc.gpsimd, w1dw[:].bitcast(I32), w1w[:].bitcast(I32))
+        deal(nc.gpsimd, w1ds[:], w1s[:])
         nc.vector.tensor_copy(two_s[:], xs[:].indirect(two_t[:]))
         nc.vector.tensor_copy(offs_s[:], xs[:].indirect(offs_t[:]))
         nc.vector.tensor_copy(two_w[:], xw[:].indirect(two_t[:]))
-        deal(nc.vector, w2ds[:], w2s[:])
-        w2dw = tile("w2dw", [P, H], U32, tag="w2s")
-        deal(nc.vector, w2dw[:].bitcast(I32), w2w[:].bitcast(I32))
-        offs_w = tile("offs_w", [P, S], U32, tag="w2w")
         nc.vector.tensor_copy(offs_w[:], xw[:].indirect(offs_t[:]))
         nc.vector.tensor_copy(cand_s0[:], xs[:].indirect(cand_t[:]))
-        deal(nc.vector, w1dw[:].bitcast(I32), w1w[:].bitcast(I32))
         deal(nc.vector, cand_s[:], cand_s0[:])
-        deal(nc.vector, w1ds[:], w1s[:])
-        cand_w = tile("cand_w", [P, C], U32, tag="w1s")
-        nc.vector.tensor_copy(cand_w[:].rearrange("p (t m) -> p m t", t=PACK), xw[:].indirect(cand_t[:]))
 
         def mm(out, lw, ls, t, rw, rs):
             m = slice(t * P, (t + 1) * P)
@@ -120,19 +118,19 @@ def tile_picked_twcjointbtrack_none_po_kernel(tc, x_words, x_scales, w1_words, w
         for t in range(PACK):
             mm(hi[t][:], w1dw, w1ds, t, offs_w[:], offs_s[:])
 
-        ga = tile("ga", [P, PACK, S], F32)
-        diff = tile("diff", [P, PACK, S], F32)
-        th = tile("th", [P, PACK, S], F32)
+        zp = tile("zp", [P, PACK, HALF], BF16)
         zb = tile("zb", [P, S * PACK], BF16)
         zw = tile("zw", [P, S], U32)
         zs = tile("zs", [P, S], U8)
 
-        def first(t, c0, n):
-            nc.vector.tensor_copy(ga[:, t, c0 : c0 + n], dwin[t][:].indirect(cols(n1_t, c0, n)))
+        def first(dst, t, c0, n):
+            nc.vector.tensor_copy(dst, dwin[t][:].indirect(cols(n1_t, c0, n)))
 
-        def second(t, c0, n):
-            nc.vector.tensor_tensor(diff[:, t, c0 : c0 + n], dwin[t][:].indirect(cols(n2_t, c0, n)), ga[:, t, c0 : c0 + n], ALU.subtract)
-            nc.scalar.activation(th[:, t, c0 : c0 + n], diff[:, t, c0 : c0 + n], ACT.Tanh, scale=-1.0)
+        def second(dst, src, t, c0, n):
+            nc.vector.tensor_tensor(dst, dwin[t][:].indirect(cols(n2_t, c0, n)), src, ALU.subtract)
+
+        def tanh(dst, src):
+            nc.scalar.activation(dst, src, ACT.Tanh, scale=-1.0)
 
         def planes(src, c0, n):
             return src[:, :, c0 : c0 + n].rearrange("p t (c i) -> p c t i", i=4)
@@ -141,7 +139,7 @@ def tile_picked_twcjointbtrack_none_po_kernel(tc, x_words, x_scales, w1_words, w
             return dst[:, c0 * PACK : (c0 + n) * PACK].rearrange("p (c i t) -> p c t i", i=4, t=PACK)
 
         def zmul(c0, n):
-            nc.vector.tensor_tensor(woven(zb, c0, n), planes(yg, c0, n), planes(th, c0, n), ALU.mult)
+            nc.vector.tensor_tensor(woven(zb, c0, n), planes(yg, c0, n), planes(thb, c0 - HALF, n), ALU.mult)
 
         def quant(w, s, b, c0, n):
             nc.vector.quantize_mx(out=w[:, c0 : c0 + n].bitcast(FP8X4), scales=s[:, c0 : c0 + n], in_=b[:, c0 * PACK : (c0 + n) * PACK])
@@ -153,26 +151,40 @@ def tile_picked_twcjointbtrack_none_po_kernel(tc, x_words, x_scales, w1_words, w
         def leave(bank, t, c0, n):
             nc.scalar.activation(swin[t][:, c0 : c0 + n], bank[t][:, c0 : c0 + n], ACT.Copy, scale=0.0625)
 
-        steps = [(t, c0, 256) for c0 in (0, 256) for t in range(PACK)]
-        first(*steps[0])
-        for i in range(len(steps)):
-            if i + 1 < len(steps):
-                first(*steps[i + 1])
-            if i == len(steps) - 1:
-                zmul(0, 256)
-            second(*steps[i])
-            if i < PACK:
-                nc.scalar.activation(yg[:, i, :], hi[i][:], ACT.Copy, scale=gs_t[:, i : i + 1])
-        quant(zw, zs, zb, 0, 256)
-        score(lo, 0, 256)
+        ga = [tile(f"ga{t}", [P, HALF], F32) for t in range(PACK)]
+        da = [tile(f"da{t}", [P, HALF], F32) for t in range(PACK)]
         for t in range(PACK):
-            leave(lo, t, 0, 256)
-        zmul(256, 128)
-        zmul(384, 128)
-        quant(zw, zs, zb, 256, 128)
-        score(hi, 256, 128)
-        quant(zw, zs, zb, 384, 128)
-        score(hi, 384, 128)
+            nc.scalar.activation(yg[:, t, :], hi[t][:], ACT.Copy, scale=gs_t[:, t : t + 1])
+        tha = tile("tha", [P, PACK, HALF], F32, tag="gs_t")
+        thb = tile("thb", [P, PACK, HALF], F32)
+        first(ga[0][:], 0, 0, HALF)
+        for t in range(PACK):
+            if t + 1 < PACK:
+                first(ga[t + 1][:], t + 1, 0, HALF)
+            second(da[t][:], ga[t][:], t, 0, HALF)
+            tanh(tha[:, t, :], da[t][:])
+        nc.gpsimd.tensor_tensor(zp[:], yg[:, :, 0:HALF], tha[:], ALU.mult)
+        nc.scalar.copy(woven(zb, 0, HALF), planes(zp, 0, HALF))
+
+        gb = [tile(f"gb{t}", [P, HALF], F32, tag=f"da{t}") for t in range(PACK)]
+        db = tile("db", [P, PACK, HALF], F32, tag="gs_t")
+        for t in range(PACK):
+            first(gb[t][:], t, HALF, HALF)
+        cand_w = tile("cand_w", [P, C], U32, tag="ga3")
+        nc.vector.tensor_copy(cand_w[:].rearrange("p (t m) -> p m t", t=PACK), xw[:].indirect(cand_t[:]))
+        for t, c0, n in [(0, 0, HALF), (1, 0, HALF), (2, 0, HALF), (3, 0, QUARTER), (3, QUARTER, QUARTER)]:
+            second(db[:, t, c0 : c0 + n], gb[t][:, c0 : c0 + n], t, HALF + c0, n)
+            tanh(thb[:, t, c0 : c0 + n], db[:, t, c0 : c0 + n])
+        quant(zw, zs, zb, 0, HALF)
+        score(lo, 0, HALF)
+        for t in range(PACK):
+            leave(lo, t, 0, HALF)
+        zmul(HALF, QUARTER)
+        zmul(HALF + QUARTER, QUARTER)
+        quant(zw, zs, zb, HALF, QUARTER)
+        score(hi, HALF, QUARTER)
+        quant(zw, zs, zb, HALF + QUARTER, QUARTER)
+        score(hi, HALF + QUARTER, QUARTER)
 
         sg = tile("sg", [P, PACK, S], F32)
         pa = tile("pa", [P, PACK, S], F32)
@@ -202,39 +214,36 @@ def tile_picked_twcjointbtrack_none_po_kernel(tc, x_words, x_scales, w1_words, w
         def store_words(c0, n):
             nc.sync.dma_start(out_words[:, c0 : c0 + n], rw[:, c0 : c0 + n].bitcast(I32))
 
-        chunks = [(0, 256), (256, 128), (384, 128)]
+        bulk = S - QUARTER
         for t in range(PACK):
-            leave(hi, t, 256, 256)
-            gate(t, *chunks[0])
-            keep(t, *chunks[0])
-            take(t, *chunks[0])
-        for t in range(PACK):
-            gate(t, *chunks[1])
-            keep(t, *chunks[1])
-            take(t, *chunks[1])
+            leave(hi, t, HALF, HALF)
+            gate(t, 0, HALF)
+            gate(t, HALF, QUARTER)
             if t == 0:
-                join(0, PACK, *chunks[0])
-                store(*chunks[0])
+                take(t, 0, HALF)
+                take(t, HALF, QUARTER)
+            else:
+                take(t, 0, bulk)
+            keep(t, 0, bulk)
         for t in range(PACK):
-            gate(t, *chunks[2])
-        nc.scalar.copy(woven(rb, *chunks[0]), planes(res, *chunks[0]))
+            gate(t, bulk, QUARTER)
+        take(0, bulk, QUARTER)
+        join(0, PACK, 0, bulk)
+        store(0, bulk)
+        nc.scalar.copy(woven(rb, 0, HALF), planes(res, 0, HALF))
+        nc.scalar.copy(woven(rb, HALF, QUARTER), planes(res, HALF, QUARTER))
         for t in range(PACK):
-            keep(t, *chunks[2])
-            take(t, *chunks[2])
-            if t == 0:
-                join(0, PACK, *chunks[1])
-                store(*chunks[1])
-                nc.scalar.copy(woven(rb, *chunks[1]), planes(res, *chunks[1]))
-            if t == 2:
-                quant(rw, rs, rb, *chunks[0])
-                store_words(*chunks[0])
-        join(0, 3, *chunks[2])
-        join(3, 4, *chunks[2])
-        quant(rw, rs, rb, *chunks[1])
-        store(*chunks[2])
-        nc.vector.tensor_copy(woven(rb, *chunks[2]), planes(res, *chunks[2]))
-        quant(rw, rs, rb, *chunks[2])
-        store_words(256, 256)
+            keep(t, bulk, QUARTER)
+            if t + 1 < PACK:
+                take(t + 1, bulk, QUARTER)
+        quant(rw, rs, rb, 0, HALF)
+        join(0, PACK, bulk, QUARTER)
+        store(bulk, QUARTER)
+        quant(rw, rs, rb, HALF, QUARTER)
+        store_words(0, bulk)
+        nc.vector.tensor_copy(woven(rb, bulk, QUARTER), planes(res, bulk, QUARTER))
+        quant(rw, rs, rb, bulk, QUARTER)
+        store_words(bulk, QUARTER)
         for q in range(4):
             eng = nc.scalar if q % 2 == 0 else nc.sync
             eng.dma_start(out_2[0][4 * q : 4 * q + 4, :].bitcast(I32), rs[32 * q : 32 * q + 4, :].bitcast(I32))

@@ -61,10 +61,10 @@ def tile_picked_twcjointbtrack_none_po_kernel(tc, x_words, x_scales, w1_words, w
             eng = nc.scalar if q < 2 else nc.sync
             eng.dma_start(xs[32 * q : 32 * q + 32, :].bitcast(I32), rows.partition_broadcast(8))
         nc.scalar.activation(warm_out[:], warm_in[:], ACT.Sigmoid)
-        xw = tile("xw", [P, T], U32)
-        nc.sync.dma_start(xw[:].bitcast(I32), words_of(x_words))
         offs_t = load_list("offs_t", offs)
         cand_t = load_list("cand_t", cand)
+        xw = tile("xw", [P, T], U32)
+        nc.sync.dma_start(xw[:].bitcast(I32), words_of(x_words))
         w2w = tile("w2w", [P, H], U32)
         nc.sync.dma_start(w2w[:].bitcast(I32), words_of(w2_words))
         load_scales(w2s, w2_scales)
@@ -85,8 +85,6 @@ def tile_picked_twcjointbtrack_none_po_kernel(tc, x_words, x_scales, w1_words, w
         two_w = tile("two_w", [P, S], U32)
         offs_s = tile("offs_s", [P, S], U8)
         offs_w = tile("offs_w", [P, S], U32)
-        cand_s0 = tile("cand_s0", [P, C], U8)
-        cand_s = tile("cand_s", [P, C], U8)
         w2ds = tile("w2ds", [P, H], U8)
         w2dw = tile("w2dw", [P, H], U32)
         w1ds = tile("w1ds", [P, H], U8)
@@ -98,9 +96,11 @@ def tile_picked_twcjointbtrack_none_po_kernel(tc, x_words, x_scales, w1_words, w
         deal(nc.gpsimd, w1ds[:], w1s[:])
         nc.vector.tensor_copy(two_s[:], xs[:].indirect(two_t[:]))
         nc.vector.tensor_copy(offs_s[:], xs[:].indirect(offs_t[:]))
+        cand_s0 = tile("cand_s0", [P, C], U8)
+        nc.vector.tensor_copy(cand_s0[:], xs[:].indirect(cand_t[:]))
         nc.vector.tensor_copy(two_w[:], xw[:].indirect(two_t[:]))
         nc.vector.tensor_copy(offs_w[:], xw[:].indirect(offs_t[:]))
-        nc.vector.tensor_copy(cand_s0[:], xs[:].indirect(cand_t[:]))
+        cand_s = tile("cand_s", [P, C], U8, tag="w2w")
         deal(nc.vector, cand_s[:], cand_s0[:])
 
         def mm(out, lw, ls, t, rw, rs):
@@ -152,21 +152,21 @@ def tile_picked_twcjointbtrack_none_po_kernel(tc, x_words, x_scales, w1_words, w
             nc.scalar.activation(swin[t][:, c0 : c0 + n], bank[t][:, c0 : c0 + n], ACT.Copy, scale=0.0625)
 
         ga = [tile(f"ga{t}", [P, HALF], F32) for t in range(PACK)]
-        da = [tile(f"da{t}", [P, HALF], F32) for t in range(PACK)]
+        spent = ["w1dw", "offs_w", "w1ds", "offs_s"]
+        da = [tile(f"da{t}", [P, HALF], F32, tag=spent[t]) for t in range(PACK)]
         for t in range(PACK):
             nc.scalar.activation(yg[:, t, :], hi[t][:], ACT.Copy, scale=gs_t[:, t : t + 1])
         tha = tile("tha", [P, PACK, HALF], F32, tag="gs_t")
         thb = tile("thb", [P, PACK, HALF], F32)
-        first(ga[0][:], 0, 0, HALF)
         for t in range(PACK):
-            if t + 1 < PACK:
-                first(ga[t + 1][:], t + 1, 0, HALF)
+            first(ga[t][:], t, 0, HALF)
+        for t in range(PACK):
             second(da[t][:], ga[t][:], t, 0, HALF)
             tanh(tha[:, t, :], da[t][:])
         nc.gpsimd.tensor_tensor(zp[:], yg[:, :, 0:HALF], tha[:], ALU.mult)
         nc.scalar.copy(woven(zb, 0, HALF), planes(zp, 0, HALF))
 
-        gb = [tile(f"gb{t}", [P, HALF], F32, tag=f"da{t}") for t in range(PACK)]
+        gb = [tile(f"gb{t}", [P, HALF], F32, tag=spent[t]) for t in range(PACK)]
         db = tile("db", [P, PACK, HALF], F32, tag="gs_t")
         for t in range(PACK):
             first(gb[t][:], t, HALF, HALF)
@@ -183,8 +183,10 @@ def tile_picked_twcjointbtrack_none_po_kernel(tc, x_words, x_scales, w1_words, w
         zmul(HALF + QUARTER, QUARTER)
         quant(zw, zs, zb, HALF, QUARTER)
         score(hi, HALF, QUARTER)
+        for t in range(PACK):
+            leave(hi, t, HALF, QUARTER)
         quant(zw, zs, zb, HALF + QUARTER, QUARTER)
-        score(hi, HALF + QUARTER, QUARTER)
+        score(lo, HALF + QUARTER, QUARTER)
 
         sg = tile("sg", [P, PACK, S], F32)
         pa = tile("pa", [P, PACK, S], F32)
@@ -208,42 +210,47 @@ def tile_picked_twcjointbtrack_none_po_kernel(tc, x_words, x_scales, w1_words, w
         def join(t0, t1, c0, n):
             nc.vector.tensor_tensor(res[:, t0:t1, c0 : c0 + n], pa[:, t0:t1, c0 : c0 + n], pu[:, t0:t1, c0 : c0 + n], ALU.subtract)
 
-        def store(c0, n):
-            nc.sync.dma_start(out_rows[:, :, c0 : c0 + n], res[:, :, c0 : c0 + n])
+        def store(t0, t1, c0, n):
+            nc.sync.dma_start(out_rows[:, t0:t1, c0 : c0 + n], res[:, t0:t1, c0 : c0 + n])
 
         def store_words(c0, n):
             nc.sync.dma_start(out_words[:, c0 : c0 + n], rw[:, c0 : c0 + n].bitcast(I32))
 
         bulk = S - QUARTER
         for t in range(PACK):
-            leave(hi, t, HALF, HALF)
+            leave(lo, t, bulk, QUARTER)
             gate(t, 0, HALF)
             gate(t, HALF, QUARTER)
             if t == 0:
-                take(t, 0, HALF)
-                take(t, HALF, QUARTER)
+                g0 = tile("g0", [P, bulk], F32)
+                nc.vector.tensor_copy(g0[:], swin[0][:].indirect(cols(n4_t, 0, bulk)))
+                nc.vector.tensor_tensor(pa[:, 0, 0:bulk], g0[:], sg[:, 0, 0:bulk], ALU.mult)
             else:
                 take(t, 0, bulk)
+            if t == 2:
+                join(0, 2, 0, bulk)
+                store(0, 2, 0, bulk)
             keep(t, 0, bulk)
         for t in range(PACK):
             gate(t, bulk, QUARTER)
         take(0, bulk, QUARTER)
-        join(0, PACK, 0, bulk)
-        store(0, bulk)
+        join(2, PACK, 0, bulk)
+        store(2, PACK, 0, bulk)
         nc.scalar.copy(woven(rb, 0, HALF), planes(res, 0, HALF))
         nc.scalar.copy(woven(rb, HALF, QUARTER), planes(res, HALF, QUARTER))
-        for t in range(PACK):
+        keep(0, bulk, QUARTER)
+        for t in range(1, PACK):
             keep(t, bulk, QUARTER)
-            if t + 1 < PACK:
-                take(t + 1, bulk, QUARTER)
+            take(t, bulk, QUARTER)
+        join(0, PACK - 1, bulk, QUARTER)
+        join(PACK - 1, PACK, bulk, QUARTER)
+        store(0, PACK, bulk, QUARTER)
         quant(rw, rs, rb, 0, HALF)
-        join(0, PACK, bulk, QUARTER)
-        store(bulk, QUARTER)
-        quant(rw, rs, rb, HALF, QUARTER)
-        store_words(0, bulk)
+        store_words(0, HALF)
         nc.vector.tensor_copy(woven(rb, bulk, QUARTER), planes(res, bulk, QUARTER))
+        quant(rw, rs, rb, HALF, QUARTER)
         quant(rw, rs, rb, bulk, QUARTER)
-        store_words(bulk, QUARTER)
+        store_words(HALF, HALF)
         for q in range(4):
             eng = nc.scalar if q % 2 == 0 else nc.sync
             eng.dma_start(out_2[0][4 * q : 4 * q + 4, :].bitcast(I32), rs[32 * q : 32 * q + 4, :].bitcast(I32))

@@ -2,7 +2,7 @@ from contextlib import ExitStack
 
 import concourse.mybir as mybir
 
-K, T, S, H, C = 512, 2048, 512, 512, 512
+T, S, H, C = 2048, 512, 512, 512
 FLOPS = 3 * 2 * 512 * 512 * 512
 
 F32 = mybir.dt.float32
@@ -17,8 +17,10 @@ ACT = mybir.ActivationFunctionType
 
 P = 128
 PACK = 4
+QUADRANTS = 4
 HALF = S // 2
 QUARTER = S // 4
+BULK = S - QUARTER
 
 
 def tile_picked_twcjointbtrack_none_po_kernel(tc, x_words, x_scales, w1_words, w1_scales, w2_words, w2_scales, gs, offs, two, n1, n2, cand, n3, n4, out_0, out_1, out_2):
@@ -28,23 +30,26 @@ def tile_picked_twcjointbtrack_none_po_kernel(tc, x_words, x_scales, w1_words, w
         sb = ctx.enter_context(tc.tile_pool(name="sb", bufs=1))
         psum = ctx.enter_context(tc.psum_pool(name="psum", bufs=1))
 
-        def tile(name, shape, dtype, tag=None):
-            return sb.tile(shape, dtype, name=name, tag=tag or name, align_bytes=64)
+        def tile(name, shape, dtype, reuse=None):
+            return sb.tile(shape, dtype, name=name, tag=reuse or name, align_bytes=64)
 
         def load_list(name, src):
-            t = lists.tile([P, S // 16], U16, name=name)
-            nc.sync.dma_start(t[:], src)
-            return t
+            offsets = lists.tile([P, S // 16], U16, name=name)
+            nc.sync.dma_start(offsets[:], src)
+            return offsets
 
-        def words_of(src):
-            return src[0].rearrange("p n t -> p (n t)").bitcast(I32)
+        def words_of(packed):
+            return packed[0].rearrange("p n t -> p (n t)").bitcast(I32)
 
-        def load_scales(dst, src):
-            for q in range(4):
-                nc.sync.dma_start(dst[32 * q : 32 * q + 4, :].bitcast(I32), src[0][4 * q : 4 * q + 4, :].bitcast(I32))
+        def scale_rows(scales, q):
+            return scales[0][4 * q : 4 * q + 4, :].bitcast(I32)
 
-        def cols(lst, c0, n):
-            return lst[:, c0 // 16 : (c0 + n) // 16]
+        def load_weight_scales(dst, scales):
+            for q in range(QUADRANTS):
+                nc.sync.dma_start(dst[32 * q : 32 * q + 4, :].bitcast(I32), scale_rows(scales, q))
+
+        def entries(offsets, c0, n):
+            return offsets[:, c0 // 16 : (c0 + n) // 16]
 
         xs = tile("xs", [P, T], U8)
         w2s = tile("w2s", [P, H], U8)
@@ -56,10 +61,9 @@ def tile_picked_twcjointbtrack_none_po_kernel(tc, x_words, x_scales, w1_words, w
         nc.vector.memset(w1s[:].bitcast(I32), 0)
 
         two_t = load_list("two_t", two)
-        for q in range(4):
-            rows = x_scales[0][4 * q : 4 * q + 4, :].bitcast(I32)
-            eng = nc.scalar if q < 2 else nc.sync
-            eng.dma_start(xs[32 * q : 32 * q + 32, :].bitcast(I32), rows.partition_broadcast(8))
+        for q in range(QUADRANTS):
+            queue = nc.scalar if q < 2 else nc.sync
+            queue.dma_start(xs[32 * q : 32 * q + 32, :].bitcast(I32), scale_rows(x_scales, q).partition_broadcast(8))
         nc.scalar.activation(warm_out[:], warm_in[:], ACT.Sigmoid)
         offs_t = load_list("offs_t", offs)
         cand_t = load_list("cand_t", cand)
@@ -67,19 +71,19 @@ def tile_picked_twcjointbtrack_none_po_kernel(tc, x_words, x_scales, w1_words, w
         nc.sync.dma_start(xw[:].bitcast(I32), words_of(x_words))
         w2w = tile("w2w", [P, H], U32)
         nc.sync.dma_start(w2w[:].bitcast(I32), words_of(w2_words))
-        load_scales(w2s, w2_scales)
+        load_weight_scales(w2s, w2_scales)
         w1w = tile("w1w", [P, H], U32)
         nc.sync.dma_start(w1w[:].bitcast(I32), words_of(w1_words))
         n1_t = load_list("n1_t", n1)
         n2_t = load_list("n2_t", n2)
-        load_scales(w1s, w1_scales)
+        load_weight_scales(w1s, w1_scales)
         gs_t = tile("gs_t", [P, PACK], F32)
         nc.sync.dma_start(gs_t[:], gs.rearrange("(p t) o -> p (t o)", t=PACK))
         n3_t = load_list("n3_t", n3)
         n4_t = load_list("n4_t", n4)
 
-        def deal(eng, dst, src):
-            eng.tensor_copy(dst.rearrange("p (t m) -> p t m", t=PACK), src.rearrange("p (m t) -> p t m", t=PACK))
+        def deal(engine, dst, src):
+            engine.tensor_copy(dst.rearrange("p (t m) -> p t m", t=PACK), src.rearrange("p (m t) -> p t m", t=PACK))
 
         two_s = tile("two_s", [P, S], U8)
         two_w = tile("two_w", [P, S], U32)
@@ -96,161 +100,177 @@ def tile_picked_twcjointbtrack_none_po_kernel(tc, x_words, x_scales, w1_words, w
         deal(nc.gpsimd, w1ds[:], w1s[:])
         nc.vector.tensor_copy(two_s[:], xs[:].indirect(two_t[:]))
         nc.vector.tensor_copy(offs_s[:], xs[:].indirect(offs_t[:]))
-        cand_s0 = tile("cand_s0", [P, C], U8)
-        nc.vector.tensor_copy(cand_s0[:], xs[:].indirect(cand_t[:]))
+        cand_listed_s = tile("cand_listed_s", [P, C], U8)
+        nc.vector.tensor_copy(cand_listed_s[:], xs[:].indirect(cand_t[:]))
         nc.vector.tensor_copy(two_w[:], xw[:].indirect(two_t[:]))
         nc.vector.tensor_copy(offs_w[:], xw[:].indirect(offs_t[:]))
-        cand_s = tile("cand_s", [P, C], U8, tag="w2w")
-        deal(nc.vector, cand_s[:], cand_s0[:])
+        cand_s = tile("cand_s", [P, C], U8, reuse="w2w")
+        deal(nc.vector, cand_s[:], cand_listed_s[:])
 
-        def mm(out, lw, ls, t, rw, rs):
+        def product(out, dealt_w, dealt_s, t, moving_w, moving_s):
             m = slice(t * P, (t + 1) * P)
-            nc.tensor.matmul_mx(out=out, lhsT=lw[:, m].bitcast(FP8X4), lhsT_scale=ls[:, m], rhs=rw.bitcast(FP8X4), rhs_scale=rs, start=True, stop=True)
+            nc.tensor.matmul_mx(
+                out=out,
+                lhsT=dealt_w[:, m].bitcast(FP8X4),
+                lhsT_scale=dealt_s[:, m],
+                rhs=moving_w.bitcast(FP8X4),
+                rhs_scale=moving_s,
+                start=True,
+                stop=True,
+            )
 
-        lo = [psum.tile([P, 512], F32, name=f"lo{t}") for t in range(PACK)]
-        hi = [psum.tile([P, 512], F32, name=f"hi{t}") for t in range(PACK)]
-        dwin = [tile(f"dwin{t}", [P, S], F32) for t in range(PACK)]
-        swin = [tile(f"swin{t}", [P, S], F32) for t in range(PACK)]
-        yg = tile("yg", [P, PACK, S], F32)
+        d_banks = [psum.tile([P, 512], F32, name=f"d_bank{t}") for t in range(PACK)]
+        y_banks = [psum.tile([P, 512], F32, name=f"y_bank{t}") for t in range(PACK)]
+        d_win = [tile(f"d_win{t}", [P, S], F32) for t in range(PACK)]
+        s_win = [tile(f"s_win{t}", [P, S], F32) for t in range(PACK)]
+        gy = tile("gy", [P, PACK, S], F32)
         for t in range(PACK):
-            mm(lo[t][:], w2dw, w2ds, t, two_w[:], two_s[:])
-            nc.scalar.copy(dwin[t][:], lo[t][:])
+            product(d_banks[t][:], w2dw, w2ds, t, two_w[:], two_s[:])
+            nc.scalar.copy(d_win[t][:], d_banks[t][:])
         for t in range(PACK):
-            mm(hi[t][:], w1dw, w1ds, t, offs_w[:], offs_s[:])
+            product(y_banks[t][:], w1dw, w1ds, t, offs_w[:], offs_s[:])
 
-        zp = tile("zp", [P, PACK, HALF], BF16)
+        z_slabs = tile("z_slabs", [P, PACK, HALF], BF16)
         zb = tile("zb", [P, S * PACK], BF16)
         zw = tile("zw", [P, S], U32)
         zs = tile("zs", [P, S], U8)
 
-        def first(dst, t, c0, n):
-            nc.vector.tensor_copy(dst, dwin[t][:].indirect(cols(n1_t, c0, n)))
+        def fetch_d1(dst, t, c0, n):
+            nc.vector.tensor_copy(dst, d_win[t][:].indirect(entries(n1_t, c0, n)))
 
-        def second(dst, src, t, c0, n):
-            nc.vector.tensor_tensor(dst, dwin[t][:].indirect(cols(n2_t, c0, n)), src, ALU.subtract)
+        def fetch_d2_less(dst, d1, t, c0, n):
+            nc.vector.tensor_tensor(dst, d_win[t][:].indirect(entries(n2_t, c0, n)), d1, ALU.subtract)
 
-        def tanh(dst, src):
+        def tanh_of_negative(dst, src):
             nc.scalar.activation(dst, src, ACT.Tanh, scale=-1.0)
 
-        def planes(src, c0, n):
+        def slab_walk(src, c0, n):
             return src[:, :, c0 : c0 + n].rearrange("p t (c i) -> p c t i", i=4)
 
-        def woven(dst, c0, n):
+        def woven_walk(dst, c0, n):
             return dst[:, c0 * PACK : (c0 + n) * PACK].rearrange("p (c i t) -> p c t i", i=4, t=PACK)
 
-        def zmul(c0, n):
-            nc.vector.tensor_tensor(woven(zb, c0, n), planes(yg, c0, n), planes(thb, c0 - HALF, n), ALU.mult)
+        def quantise(words, scales, woven, c0, n):
+            nc.vector.quantize_mx(
+                out=words[:, c0 : c0 + n].bitcast(FP8X4),
+                scales=scales[:, c0 : c0 + n],
+                in_=woven[:, c0 * PACK : (c0 + n) * PACK],
+            )
 
-        def quant(w, s, b, c0, n):
-            nc.vector.quantize_mx(out=w[:, c0 : c0 + n].bitcast(FP8X4), scales=s[:, c0 : c0 + n], in_=b[:, c0 * PACK : (c0 + n) * PACK])
-
-        def score(bank, c0, n):
+        def score(banks, c0, n):
             for t in range(PACK):
-                mm(bank[t][:, c0 : c0 + n], cand_w, cand_s, t, zw[:, c0 : c0 + n], zs[:, c0 : c0 + n])
+                product(banks[t][:, c0 : c0 + n], cand_w, cand_s, t, zw[:, c0 : c0 + n], zs[:, c0 : c0 + n])
 
-        def leave(bank, t, c0, n):
-            nc.scalar.activation(swin[t][:, c0 : c0 + n], bank[t][:, c0 : c0 + n], ACT.Copy, scale=0.0625)
+        def leave_psum(banks, t, c0, n):
+            nc.scalar.activation(s_win[t][:, c0 : c0 + n], banks[t][:, c0 : c0 + n], ACT.Copy, scale=0.0625)
 
-        ga = [tile(f"ga{t}", [P, HALF], F32) for t in range(PACK)]
-        spent = ["w1dw", "offs_w", "w1ds", "offs_s"]
-        da = [tile(f"da{t}", [P, HALF], F32, tag=spent[t]) for t in range(PACK)]
+        d1_a = [tile(f"d1_a{t}", [P, HALF], F32) for t in range(PACK)]
+        y_operands = ["w1dw", "offs_w", "w1ds", "offs_s"]
+        diff_a = [tile(f"diff_a{t}", [P, HALF], F32, reuse=y_operands[t]) for t in range(PACK)]
         for t in range(PACK):
-            nc.scalar.activation(yg[:, t, :], hi[t][:], ACT.Copy, scale=gs_t[:, t : t + 1])
-        tha = tile("tha", [P, PACK, HALF], F32, tag="gs_t")
-        thb = tile("thb", [P, PACK, HALF], F32)
+            nc.scalar.activation(gy[:, t, :], y_banks[t][:], ACT.Copy, scale=gs_t[:, t : t + 1])
+        tanh_a = tile("tanh_a", [P, PACK, HALF], F32, reuse="gs_t")
+        tanh_b = tile("tanh_b", [P, PACK, HALF], F32)
         for t in range(PACK):
-            first(ga[t][:], t, 0, HALF)
+            fetch_d1(d1_a[t][:], t, 0, HALF)
         for t in range(PACK):
-            second(da[t][:], ga[t][:], t, 0, HALF)
-            tanh(tha[:, t, :], da[t][:])
-        nc.gpsimd.tensor_tensor(zp[:], yg[:, :, 0:HALF], tha[:], ALU.mult)
-        nc.scalar.copy(woven(zb, 0, HALF), planes(zp, 0, HALF))
+            fetch_d2_less(diff_a[t][:], d1_a[t][:], t, 0, HALF)
+            tanh_of_negative(tanh_a[:, t, :], diff_a[t][:])
+        nc.gpsimd.tensor_tensor(z_slabs[:], gy[:, :, 0:HALF], tanh_a[:], ALU.mult)
+        nc.scalar.copy(woven_walk(zb, 0, HALF), slab_walk(z_slabs, 0, HALF))
 
-        gb = [tile(f"gb{t}", [P, HALF], F32, tag=spent[t]) for t in range(PACK)]
-        db = tile("db", [P, PACK, HALF], F32, tag="gs_t")
+        d1_b = [tile(f"d1_b{t}", [P, HALF], F32, reuse=y_operands[t]) for t in range(PACK)]
+        diff_b = tile("diff_b", [P, PACK, HALF], F32, reuse="gs_t")
         for t in range(PACK):
-            first(gb[t][:], t, HALF, HALF)
-        cand_w = tile("cand_w", [P, C], U32, tag="ga3")
+            fetch_d1(d1_b[t][:], t, HALF, HALF)
+        cand_w = tile("cand_w", [P, C], U32, reuse=f"d1_a{PACK - 1}")
         nc.vector.tensor_copy(cand_w[:].rearrange("p (t m) -> p m t", t=PACK), xw[:].indirect(cand_t[:]))
-        for t, c0, n in [(0, 0, HALF), (1, 0, HALF), (2, 0, HALF), (3, 0, QUARTER), (3, QUARTER, QUARTER)]:
-            second(db[:, t, c0 : c0 + n], gb[t][:, c0 : c0 + n], t, HALF + c0, n)
-            tanh(thb[:, t, c0 : c0 + n], db[:, t, c0 : c0 + n])
-        quant(zw, zs, zb, 0, HALF)
-        score(lo, 0, HALF)
-        for t in range(PACK):
-            leave(lo, t, 0, HALF)
-        zmul(HALF, QUARTER)
-        zmul(HALF + QUARTER, QUARTER)
-        quant(zw, zs, zb, HALF, QUARTER)
-        score(hi, HALF, QUARTER)
-        for t in range(PACK):
-            leave(hi, t, HALF, QUARTER)
-        quant(zw, zs, zb, HALF + QUARTER, QUARTER)
-        score(lo, HALF + QUARTER, QUARTER)
+        pieces = [(t, 0, HALF) for t in range(PACK - 1)] + [(PACK - 1, c0, QUARTER) for c0 in (0, QUARTER)]
+        for t, c0, n in pieces:
+            fetch_d2_less(diff_b[:, t, c0 : c0 + n], d1_b[t][:, c0 : c0 + n], t, HALF + c0, n)
+            tanh_of_negative(tanh_b[:, t, c0 : c0 + n], diff_b[:, t, c0 : c0 + n])
 
-        sg = tile("sg", [P, PACK, S], F32)
-        pa = tile("pa", [P, PACK, S], F32)
-        pu = tile("pu", [P, PACK, S], F32)
+        quantise(zw, zs, zb, 0, HALF)
+        score(d_banks, 0, HALF)
+        for t in range(PACK):
+            leave_psum(d_banks, t, 0, HALF)
+        for c0 in (HALF, BULK):
+            nc.vector.tensor_tensor(woven_walk(zb, c0, QUARTER), slab_walk(gy, c0, QUARTER), slab_walk(tanh_b, c0 - HALF, QUARTER), ALU.mult)
+        quantise(zw, zs, zb, HALF, QUARTER)
+        score(y_banks, HALF, QUARTER)
+        leave_psum(y_banks, 0, HALF, QUARTER)
+        quantise(zw, zs, zb, BULK, QUARTER)
+        score(d_banks[:1] + y_banks[1:], BULK, QUARTER)
+
+        gate = tile("gate", [P, PACK, S], F32)
+        taken = tile("taken", [P, PACK, S], F32)
+        kept = tile("kept", [P, PACK, S], F32)
         res = tile("res", [P, PACK, S], F32)
         rb = tile("rb", [P, S * PACK], BF16)
         rw = tile("rw", [P, S], U32)
         rs = tile("rs", [P, S], U8)
-        out_rows = out_0.rearrange("(p t) c -> p t c", t=PACK)
+        out_slabs = out_0.rearrange("(p t) c -> p t c", t=PACK)
         out_words = words_of(out_1)
 
-        def gate(t, c0, n):
-            nc.scalar.activation(sg[:, t, c0 : c0 + n], swin[t][:].indirect(cols(n3_t, c0, n)), ACT.Sigmoid)
+        def fetch_gate(t, c0, n):
+            nc.scalar.activation(gate[:, t, c0 : c0 + n], s_win[t][:].indirect(entries(n3_t, c0, n)), ACT.Sigmoid)
 
         def keep(t, c0, n):
-            nc.vector.scalar_tensor_tensor(pu[:, t, c0 : c0 + n], sg[:, t, c0 : c0 + n], 1.0, swin[t][:, c0 : c0 + n], ALU.subtract, ALU.mult)
+            nc.vector.scalar_tensor_tensor(kept[:, t, c0 : c0 + n], gate[:, t, c0 : c0 + n], 1.0, s_win[t][:, c0 : c0 + n], ALU.subtract, ALU.mult)
 
         def take(t, c0, n):
-            nc.vector.tensor_tensor(pa[:, t, c0 : c0 + n], swin[t][:].indirect(cols(n4_t, c0, n)), sg[:, t, c0 : c0 + n], ALU.mult)
+            nc.vector.tensor_tensor(taken[:, t, c0 : c0 + n], s_win[t][:].indirect(entries(n4_t, c0, n)), gate[:, t, c0 : c0 + n], ALU.mult)
 
         def join(t0, t1, c0, n):
-            nc.vector.tensor_tensor(res[:, t0:t1, c0 : c0 + n], pa[:, t0:t1, c0 : c0 + n], pu[:, t0:t1, c0 : c0 + n], ALU.subtract)
+            nc.vector.tensor_tensor(res[:, t0:t1, c0 : c0 + n], taken[:, t0:t1, c0 : c0 + n], kept[:, t0:t1, c0 : c0 + n], ALU.subtract)
 
         def store(t0, t1, c0, n):
-            nc.sync.dma_start(out_rows[:, t0:t1, c0 : c0 + n], res[:, t0:t1, c0 : c0 + n])
+            nc.sync.dma_start(out_slabs[:, t0:t1, c0 : c0 + n], res[:, t0:t1, c0 : c0 + n])
 
         def store_words(c0, n):
             nc.sync.dma_start(out_words[:, c0 : c0 + n], rw[:, c0 : c0 + n].bitcast(I32))
 
-        bulk = S - QUARTER
+        early = 2
+        s4 = [tile(f"s4_{t}", [P, BULK], F32) for t in range(early)]
         for t in range(PACK):
-            leave(lo, t, bulk, QUARTER)
-            gate(t, 0, HALF)
-            gate(t, HALF, QUARTER)
             if t == 0:
-                g0 = tile("g0", [P, bulk], F32)
-                nc.vector.tensor_copy(g0[:], swin[0][:].indirect(cols(n4_t, 0, bulk)))
-                nc.vector.tensor_tensor(pa[:, 0, 0:bulk], g0[:], sg[:, 0, 0:bulk], ALU.mult)
+                leave_psum(d_banks, t, BULK, QUARTER)
             else:
-                take(t, 0, bulk)
-            if t == 2:
-                join(0, 2, 0, bulk)
-                store(0, 2, 0, bulk)
-            keep(t, 0, bulk)
+                leave_psum(y_banks, t, HALF, HALF)
+            fetch_gate(t, 0, HALF)
+            fetch_gate(t, HALF, QUARTER)
+        for t in range(early):
+            nc.vector.tensor_copy(s4[t][:], s_win[t][:].indirect(entries(n4_t, 0, BULK)))
+            keep(t, 0, BULK)
+            nc.vector.tensor_tensor(taken[:, t, 0:BULK], s4[t][:], gate[:, t, 0:BULK], ALU.mult)
+        join(0, 1, 0, BULK)
+        take(2, 0, BULK)
+        join(1, 2, 0, BULK)
+        store(0, 2, 0, BULK)
+        keep(2, 0, BULK)
+        take(3, 0, BULK)
+        keep(3, 0, BULK)
         for t in range(PACK):
-            gate(t, bulk, QUARTER)
-        take(0, bulk, QUARTER)
-        join(2, PACK, 0, bulk)
-        store(2, PACK, 0, bulk)
-        nc.scalar.copy(woven(rb, 0, HALF), planes(res, 0, HALF))
-        nc.scalar.copy(woven(rb, HALF, QUARTER), planes(res, HALF, QUARTER))
-        keep(0, bulk, QUARTER)
+            fetch_gate(t, BULK, QUARTER)
+        take(0, BULK, QUARTER)
+        join(2, PACK, 0, BULK)
+        store(2, PACK, 0, BULK)
+        nc.scalar.copy(woven_walk(rb, 0, HALF), slab_walk(res, 0, HALF))
+        nc.scalar.copy(woven_walk(rb, HALF, QUARTER), slab_walk(res, HALF, QUARTER))
+
+        keep(0, BULK, QUARTER)
         for t in range(1, PACK):
-            keep(t, bulk, QUARTER)
-            take(t, bulk, QUARTER)
-        join(0, PACK - 1, bulk, QUARTER)
-        join(PACK - 1, PACK, bulk, QUARTER)
-        store(0, PACK, bulk, QUARTER)
-        quant(rw, rs, rb, 0, HALF)
+            keep(t, BULK, QUARTER)
+            take(t, BULK, QUARTER)
+        join(0, PACK - 1, BULK, QUARTER)
+        join(PACK - 1, PACK, BULK, QUARTER)
+        store(0, PACK, BULK, QUARTER)
+        quantise(rw, rs, rb, 0, HALF)
         store_words(0, HALF)
-        nc.vector.tensor_copy(woven(rb, bulk, QUARTER), planes(res, bulk, QUARTER))
-        quant(rw, rs, rb, HALF, QUARTER)
-        quant(rw, rs, rb, bulk, QUARTER)
+        nc.vector.tensor_copy(woven_walk(rb, BULK, QUARTER), slab_walk(res, BULK, QUARTER))
+        quantise(rw, rs, rb, HALF, QUARTER)
+        quantise(rw, rs, rb, BULK, QUARTER)
         store_words(HALF, HALF)
-        for q in range(4):
-            eng = nc.scalar if q % 2 == 0 else nc.sync
-            eng.dma_start(out_2[0][4 * q : 4 * q + 4, :].bitcast(I32), rs[32 * q : 32 * q + 4, :].bitcast(I32))
+        for q in range(QUADRANTS):
+            queue = nc.scalar if q % 2 == 0 else nc.sync
+            queue.dma_start(scale_rows(out_2, q), rs[32 * q : 32 * q + 4, :].bitcast(I32))

from contextlib import ExitStack

import concourse.mybir as mybir

T, S, H, C = 2048, 512, 512, 512
FLOPS = 3 * 2 * 512 * 512 * 512

F32 = mybir.dt.float32
BF16 = mybir.dt.bfloat16
I32 = mybir.dt.int32
U32 = mybir.dt.uint32
U16 = mybir.dt.uint16
U8 = mybir.dt.uint8
FP8X4 = mybir.dt.float8_e4m3fn_x4
ALU = mybir.AluOpType
ACT = mybir.ActivationFunctionType

P = 128
PACK = 4
QUADRANTS = 4
HALF = S // 2
QUARTER = S // 4
BULK = S - QUARTER


def tile_picked_twcjointbtrack_none_po_kernel(tc, x_words, x_scales, w1_words, w1_scales, w2_words, w2_scales, gs, offs, two, n1, n2, cand, n3, n4, out_0, out_1, out_2):
    nc = tc.nc
    with ExitStack() as ctx:
        lists = ctx.enter_context(tc.tile_pool(name="lists", bufs=1))
        sb = ctx.enter_context(tc.tile_pool(name="sb", bufs=1))
        psum = ctx.enter_context(tc.psum_pool(name="psum", bufs=1))

        def tile(name, shape, dtype, reuse=None):
            return sb.tile(shape, dtype, name=name, tag=reuse or name, align_bytes=64)

        def load_list(name, src):
            offsets = lists.tile([P, S // 16], U16, name=name)
            nc.sync.dma_start(offsets[:], src)
            return offsets

        def words_of(packed):
            return packed[0].rearrange("p n t -> p (n t)").bitcast(I32)

        def scale_rows(scales, q):
            return scales[0][4 * q : 4 * q + 4, :].bitcast(I32)

        def load_weight_scales(dst, scales):
            for q in range(QUADRANTS):
                nc.sync.dma_start(dst[32 * q : 32 * q + 4, :].bitcast(I32), scale_rows(scales, q))

        def entries(offsets, c0, n):
            return offsets[:, c0 // 16 : (c0 + n) // 16]

        xs = tile("xs", [P, T], U8)
        w2s = tile("w2s", [P, H], U8)
        w1s = tile("w1s", [P, H], U8)
        warm_in = tile("warm_in", [P, 1], F32)
        warm_out = tile("warm_out", [P, 1], F32)
        nc.vector.memset(warm_in[:], 0.0)
        nc.vector.memset(w2s[:].bitcast(I32), 0)
        nc.vector.memset(w1s[:].bitcast(I32), 0)

        two_t = load_list("two_t", two)
        for q in range(QUADRANTS):
            queue = nc.scalar if q < 2 else nc.sync
            queue.dma_start(xs[32 * q : 32 * q + 32, :].bitcast(I32), scale_rows(x_scales, q).partition_broadcast(8))
        nc.scalar.activation(warm_out[:], warm_in[:], ACT.Sigmoid)
        offs_t = load_list("offs_t", offs)
        cand_t = load_list("cand_t", cand)
        xw = tile("xw", [P, T], U32)
        nc.sync.dma_start(xw[:].bitcast(I32), words_of(x_words))
        w2w = tile("w2w", [P, H], U32)
        nc.sync.dma_start(w2w[:].bitcast(I32), words_of(w2_words))
        load_weight_scales(w2s, w2_scales)
        w1w = tile("w1w", [P, H], U32)
        nc.sync.dma_start(w1w[:].bitcast(I32), words_of(w1_words))
        n1_t = load_list("n1_t", n1)
        n2_t = load_list("n2_t", n2)
        load_weight_scales(w1s, w1_scales)
        gs_t = tile("gs_t", [P, PACK], F32)
        nc.sync.dma_start(gs_t[:], gs.rearrange("(p t) o -> p (t o)", t=PACK))
        n3_t = load_list("n3_t", n3)
        n4_t = load_list("n4_t", n4)

        def deal(engine, dst, src):
            engine.tensor_copy(dst.rearrange("p (t m) -> p t m", t=PACK), src.rearrange("p (m t) -> p t m", t=PACK))

        two_s = tile("two_s", [P, S], U8)
        two_w = tile("two_w", [P, S], U32)
        offs_s = tile("offs_s", [P, S], U8)
        offs_w = tile("offs_w", [P, S], U32)
        w2ds = tile("w2ds", [P, H], U8)
        w2dw = tile("w2dw", [P, H], U32)
        w1ds = tile("w1ds", [P, H], U8)
        w1dw = tile("w1dw", [P, H], U32)

        deal(nc.gpsimd, w2dw[:].bitcast(I32), w2w[:].bitcast(I32))
        deal(nc.gpsimd, w2ds[:], w2s[:])
        deal(nc.gpsimd, w1dw[:].bitcast(I32), w1w[:].bitcast(I32))
        deal(nc.gpsimd, w1ds[:], w1s[:])
        nc.vector.tensor_copy(two_s[:], xs[:].indirect(two_t[:]))
        nc.vector.tensor_copy(offs_s[:], xs[:].indirect(offs_t[:]))
        cand_listed_s = tile("cand_listed_s", [P, C], U8)
        nc.vector.tensor_copy(cand_listed_s[:], xs[:].indirect(cand_t[:]))
        nc.vector.tensor_copy(two_w[:], xw[:].indirect(two_t[:]))
        nc.vector.tensor_copy(offs_w[:], xw[:].indirect(offs_t[:]))
        cand_s = tile("cand_s", [P, C], U8, reuse="w2w")
        deal(nc.vector, cand_s[:], cand_listed_s[:])

        def product(out, dealt_w, dealt_s, t, moving_w, moving_s):
            m = slice(t * P, (t + 1) * P)
            nc.tensor.matmul_mx(
                out=out,
                lhsT=dealt_w[:, m].bitcast(FP8X4),
                lhsT_scale=dealt_s[:, m],
                rhs=moving_w.bitcast(FP8X4),
                rhs_scale=moving_s,
                start=True,
                stop=True,
            )

        d_banks = [psum.tile([P, 512], F32, name=f"d_bank{t}") for t in range(PACK)]
        y_banks = [psum.tile([P, 512], F32, name=f"y_bank{t}") for t in range(PACK)]
        d_win = [tile(f"d_win{t}", [P, S], F32) for t in range(PACK)]
        s_win = [tile(f"s_win{t}", [P, S], F32) for t in range(PACK)]
        gy = tile("gy", [P, PACK, S], F32)
        for t in range(PACK):
            product(d_banks[t][:], w2dw, w2ds, t, two_w[:], two_s[:])
            nc.scalar.copy(d_win[t][:], d_banks[t][:])
        for t in range(PACK):
            product(y_banks[t][:], w1dw, w1ds, t, offs_w[:], offs_s[:])

        z_slabs = tile("z_slabs", [P, PACK, HALF], BF16)
        zb = tile("zb", [P, S * PACK], BF16)
        zw = tile("zw", [P, S], U32)
        zs = tile("zs", [P, S], U8)

        def fetch_d1(dst, t, c0, n):
            nc.vector.tensor_copy(dst, d_win[t][:].indirect(entries(n1_t, c0, n)))

        def fetch_d2_less(dst, d1, t, c0, n):
            nc.vector.tensor_tensor(dst, d_win[t][:].indirect(entries(n2_t, c0, n)), d1, ALU.subtract)

        def tanh_of_negative(dst, src):
            nc.scalar.activation(dst, src, ACT.Tanh, scale=-1.0)

        def slab_walk(src, c0, n):
            return src[:, :, c0 : c0 + n].rearrange("p t (c i) -> p c t i", i=4)

        def woven_walk(dst, c0, n):
            return dst[:, c0 * PACK : (c0 + n) * PACK].rearrange("p (c i t) -> p c t i", i=4, t=PACK)

        def quantise(words, scales, woven, c0, n):
            nc.vector.quantize_mx(
                out=words[:, c0 : c0 + n].bitcast(FP8X4),
                scales=scales[:, c0 : c0 + n],
                in_=woven[:, c0 * PACK : (c0 + n) * PACK],
            )

        def score(banks, c0, n):
            for t in range(PACK):
                product(banks[t][:, c0 : c0 + n], cand_w, cand_s, t, zw[:, c0 : c0 + n], zs[:, c0 : c0 + n])

        def leave_psum(banks, t, c0, n):
            nc.scalar.activation(s_win[t][:, c0 : c0 + n], banks[t][:, c0 : c0 + n], ACT.Copy, scale=0.0625)

        d1_a = [tile(f"d1_a{t}", [P, HALF], F32) for t in range(PACK)]
        y_operands = ["w1dw", "offs_w", "w1ds", "offs_s"]
        diff_a = [tile(f"diff_a{t}", [P, HALF], F32, reuse=y_operands[t]) for t in range(PACK)]
        for t in range(PACK):
            nc.scalar.activation(gy[:, t, :], y_banks[t][:], ACT.Copy, scale=gs_t[:, t : t + 1])
        tanh_a = tile("tanh_a", [P, PACK, HALF], F32, reuse="gs_t")
        tanh_b = tile("tanh_b", [P, PACK, HALF], F32)
        for t in range(PACK):
            fetch_d1(d1_a[t][:], t, 0, HALF)
        for t in range(PACK):
            fetch_d2_less(diff_a[t][:], d1_a[t][:], t, 0, HALF)
            tanh_of_negative(tanh_a[:, t, :], diff_a[t][:])
        nc.gpsimd.tensor_tensor(z_slabs[:], gy[:, :, 0:HALF], tanh_a[:], ALU.mult)
        nc.scalar.copy(woven_walk(zb, 0, HALF), slab_walk(z_slabs, 0, HALF))

        d1_b = [tile(f"d1_b{t}", [P, HALF], F32, reuse=y_operands[t]) for t in range(PACK)]
        diff_b = tile("diff_b", [P, PACK, HALF], F32, reuse="gs_t")
        for t in range(PACK):
            fetch_d1(d1_b[t][:], t, HALF, HALF)
        cand_w = tile("cand_w", [P, C], U32, reuse=f"d1_a{PACK - 1}")
        nc.vector.tensor_copy(cand_w[:].rearrange("p (t m) -> p m t", t=PACK), xw[:].indirect(cand_t[:]))
        pieces = [(t, 0, HALF) for t in range(PACK - 1)] + [(PACK - 1, c0, QUARTER) for c0 in (0, QUARTER)]
        for t, c0, n in pieces:
            fetch_d2_less(diff_b[:, t, c0 : c0 + n], d1_b[t][:, c0 : c0 + n], t, HALF + c0, n)
            tanh_of_negative(tanh_b[:, t, c0 : c0 + n], diff_b[:, t, c0 : c0 + n])

        quantise(zw, zs, zb, 0, HALF)
        score(d_banks, 0, HALF)
        for t in range(PACK):
            leave_psum(d_banks, t, 0, HALF)
        for c0 in (HALF, BULK):
            nc.vector.tensor_tensor(woven_walk(zb, c0, QUARTER), slab_walk(gy, c0, QUARTER), slab_walk(tanh_b, c0 - HALF, QUARTER), ALU.mult)
        quantise(zw, zs, zb, HALF, QUARTER)
        score(y_banks, HALF, QUARTER)
        leave_psum(y_banks, 0, HALF, QUARTER)
        quantise(zw, zs, zb, BULK, QUARTER)
        score(d_banks[:1] + y_banks[1:], BULK, QUARTER)

        gate = tile("gate", [P, PACK, S], F32)
        taken = tile("taken", [P, PACK, S], F32)
        kept = tile("kept", [P, PACK, S], F32)
        res = tile("res", [P, PACK, S], F32)
        rb = tile("rb", [P, S * PACK], BF16)
        rw = tile("rw", [P, S], U32)
        rs = tile("rs", [P, S], U8)
        out_slabs = out_0.rearrange("(p t) c -> p t c", t=PACK)
        out_words = words_of(out_1)

        def fetch_gate(t, c0, n):
            nc.scalar.activation(gate[:, t, c0 : c0 + n], s_win[t][:].indirect(entries(n3_t, c0, n)), ACT.Sigmoid)

        def keep(t, c0, n):
            nc.vector.scalar_tensor_tensor(kept[:, t, c0 : c0 + n], gate[:, t, c0 : c0 + n], 1.0, s_win[t][:, c0 : c0 + n], ALU.subtract, ALU.mult)

        def take(t, c0, n):
            nc.vector.tensor_tensor(taken[:, t, c0 : c0 + n], s_win[t][:].indirect(entries(n4_t, c0, n)), gate[:, t, c0 : c0 + n], ALU.mult)

        def join(t0, t1, c0, n):
            nc.vector.tensor_tensor(res[:, t0:t1, c0 : c0 + n], taken[:, t0:t1, c0 : c0 + n], kept[:, t0:t1, c0 : c0 + n], ALU.subtract)

        def store(t0, t1, c0, n):
            nc.sync.dma_start(out_slabs[:, t0:t1, c0 : c0 + n], res[:, t0:t1, c0 : c0 + n])

        def store_words(c0, n):
            nc.sync.dma_start(out_words[:, c0 : c0 + n], rw[:, c0 : c0 + n].bitcast(I32))

        early = 2
        s4 = [tile(f"s4_{t}", [P, BULK], F32) for t in range(early)]
        for t in range(PACK):
            if t == 0:
                leave_psum(d_banks, t, BULK, QUARTER)
            else:
                leave_psum(y_banks, t, HALF, HALF)
            fetch_gate(t, 0, HALF)
            fetch_gate(t, HALF, QUARTER)
        for t in range(early):
            nc.vector.tensor_copy(s4[t][:], s_win[t][:].indirect(entries(n4_t, 0, BULK)))
            keep(t, 0, BULK)
            nc.vector.tensor_tensor(taken[:, t, 0:BULK], s4[t][:], gate[:, t, 0:BULK], ALU.mult)
        join(0, 1, 0, BULK)
        take(2, 0, BULK)
        join(1, 2, 0, BULK)
        store(0, 2, 0, BULK)
        keep(2, 0, BULK)
        take(3, 0, BULK)
        keep(3, 0, BULK)
        for t in range(PACK):
            fetch_gate(t, BULK, QUARTER)
        take(0, BULK, QUARTER)
        join(2, PACK, 0, BULK)
        store(2, PACK, 0, BULK)
        nc.scalar.copy(woven_walk(rb, 0, HALF), slab_walk(res, 0, HALF))
        nc.scalar.copy(woven_walk(rb, HALF, QUARTER), slab_walk(res, HALF, QUARTER))

        keep(0, BULK, QUARTER)
        for t in range(1, PACK):
            keep(t, BULK, QUARTER)
            take(t, BULK, QUARTER)
        join(0, PACK - 1, BULK, QUARTER)
        join(PACK - 1, PACK, BULK, QUARTER)
        store(0, PACK, BULK, QUARTER)
        quantise(rw, rs, rb, 0, HALF)
        store_words(0, HALF)
        nc.vector.tensor_copy(woven_walk(rb, BULK, QUARTER), slab_walk(res, BULK, QUARTER))
        quantise(rw, rs, rb, HALF, QUARTER)
        quantise(rw, rs, rb, BULK, QUARTER)
        store_words(HALF, HALF)
        for q in range(QUADRANTS):
            queue = nc.scalar if q % 2 == 0 else nc.sync
            queue.dma_start(scale_rows(out_2, q), rs[32 * q : 32 * q + 4, :].bitcast(I32))
